import numpy as np
import ml_dtypes


def mxq(x, axis, fmt="e4m3"):
    dtype, down = {"e4m3": (ml_dtypes.float8_e4m3fn, 7), "e5m2": (ml_dtypes.float8_e5m2, 14)}[fmt]
    v = np.moveaxis(np.asarray(x, np.float32).astype(ml_dtypes.bfloat16).astype(np.float64), axis, -1)
    blocks = v.reshape(v.shape[:-1] + (-1, 32))
    amax = np.abs(blocks).max(-1, keepdims=True)
    byte = np.maximum(np.where(amax > 0, np.frexp(amax)[1] - 1 + 127, 0) - down, 1)
    scale = np.exp2(byte - 127.0)
    codes = (blocks / scale).astype(np.float32).astype(dtype).astype(np.float64)
    return np.moveaxis((codes * scale).reshape(v.shape), -1, axis)


WIDE = False


def mx_kscale(k):
    if not WIDE:
        return np.ones(k)
    levels = np.array([10, -10, 5, -5, 0])
    if k % 512:
        return np.exp2(np.random.permutation(np.resize(levels, k // 32))).repeat(32)
    a = np.empty((k // 512, 16))
    for p in range(k // 512):
        a[p, :8] = np.random.permutation(np.resize(levels, 8))
        for g in range(8):
            far = levels[np.abs(levels - a[p, g]) >= 10]
            a[p, g + 8] = far[np.random.randint(len(far))]
    return np.exp2(a.ravel()).repeat(32)


def f64(x):
    return np.asarray(x).astype(np.float64)


def striped(idx):
    return np.tile(idx.reshape(-1, 16).T, (8, 1)).astype(np.uint16)


def unstriped(offs):
    return offs[:16].T.reshape(-1).astype(np.int64)


def pack_weight(w):
    k, n = w.shape
    w = f64(np.asarray(w, np.float32).astype(ml_dtypes.bfloat16)).reshape(k // 32, 32, n)
    amax = np.abs(w).max(1)
    byte = np.clip(np.where(amax > 0, np.frexp(amax)[1] - 1 + 127 - 7, 1), 1, 254)
    scaled = (w * np.exp2(127.0 - byte)[:, None, :]).reshape(k, n).astype(np.float32)
    words = np.ascontiguousarray(scaled.reshape(k // 512, 128, 4, n).transpose(0, 1, 3, 2)).astype(ml_dtypes.float8_e4m3fn).view(np.uint8)
    return words, np.ascontiguousarray(byte.astype(np.uint8).reshape(k // 512, 16, n))


def unpack_weight(words, scales):
    g, p, n, _ = words.shape
    vals = np.ascontiguousarray(words).view(ml_dtypes.float8_e4m3fn).astype(np.float64) * np.repeat(np.exp2(scales.astype(np.float64) - 127.0), 8, axis=1)[..., None]
    return vals.transpose(0, 1, 3, 2).reshape(g * 512, n)

def planes(y):
    n, m = y.shape
    v = y.astype(np.float32).astype(ml_dtypes.bfloat16).astype(np.float64).reshape(n // 32, 32, m)
    top = np.abs(v).max(1)
    byte = np.clip(np.where(top > 0, np.frexp(top)[1] - 1 + 127 - 7, 1), 1, 254)
    codes = (v * np.exp2(127.0 - byte)[:, None, :]).reshape(n, m).astype(np.float32).astype(ml_dtypes.float8_e4m3fn).view(np.uint8)
    words = codes.reshape(n // 512, 128, 4, m).transpose(0, 1, 3, 2)
    return np.ascontiguousarray(words), np.ascontiguousarray(byte.astype(np.uint8).reshape(n // 512, 16, m))


K, T, S, V, H = 512, 1024, 768, 256, 512


def setup_inputs():
    n = np.random.standard_normal
    s = mx_kscale(K)[:, None]
    u = mx_kscale(H)
    packed_xT = pack_weight(n((K, T)) * s)
    packed_w4 = pack_weight(n((H, H)) / np.sqrt(H) / u[:, None])
    return {
        "x_words": packed_xT[0],
        "x_scales": packed_xT[1],
        "w1": (n((K, H)) / np.sqrt(K) / s * u).astype(np.float32),
        "w2": (n((K, H)) / np.sqrt(K) / s).astype(np.float32),
        "w3": (n((K, H)) / np.sqrt(K) / s).astype(np.float32),
        "w4_words": packed_w4[0],
        "w4_scales": packed_w4[1],
        "offs": striped(np.random.permutation(T)[:S]),
    }


def reference(x_words, x_scales, w1, w2, w3, w4_words, w4_scales, offs):
    xq = unpack_weight(x_words, x_scales)[:, unstriped(offs)]
    z = (((mxq(f64(w1), 0, "e4m3").T @ xq[:, :V])) * ((mxq(f64(w2), 0, "e4m3").T @ xq[:, V:2 * V]))) * ((mxq(f64(w3), 0, "e4m3").T @ xq[:, 2 * V:3 * V]))
    out_0 = unpack_weight(w4_words, w4_scales).T @ mxq(z, 0, "e4m3")
    return (out_0,) + planes(out_0)

@@ -1,0 +1,180 @@
+from contextlib import ExitStack
+
+import concourse.mybir as mybir
+
+K, T, S, V, H = 512, 1024, 768, 256, 512
+FLOPS = 3 * 2 * K * H * V + 2 * H * H * V
+
+F32 = mybir.dt.float32
+BF16 = mybir.dt.bfloat16
+I32 = mybir.dt.int32
+U32 = mybir.dt.uint32
+U16 = mybir.dt.uint16
+U8 = mybir.dt.uint8
+FP8X4 = mybir.dt.float8_e4m3fn_x4
+MULT = mybir.AluOpType.mult
+
+P = 128
+PACK = 4
+HALF = V // 2
+LIST_COLS = V // 16
+
+
+def tile_picked_trilin_none_po_kernel(
+    tc, x_words, x_scales, w1, w2, w3, w4_words, w4_scales, offs, out_0, out_1, out_2
+):
+    nc = tc.nc
+    with ExitStack() as ctx:
+        keep = ctx.enter_context(tc.tile_pool(name="keep", bufs=1))
+        psum = ctx.enter_context(tc.psum_pool(name="psum", bufs=1))
+
+        def sb(name, shape, dtype):
+            return keep.tile(shape, dtype, name=name, align_bytes=64)
+
+        def bank(name, index, slots):
+            return psum.tile([P, slots, HALF], F32, name=name, tag="bank%d" % index)
+
+        offsets = keep.tile([P, S // 16], U16, name="offsets")
+        nc.sync.dma_start(offsets[:], offs)
+
+        def load_scale_rows(queue, name, rows, width):
+            plane = sb(name, [P, width], U8)
+            nc.vector.memset(plane[:].bitcast(I32), 0)
+            for q in range(4):
+                queue.dma_start(plane[32 * q : 32 * q + 4, :].bitcast(I32), rows[0, 4 * q : 4 * q + 4, :].bitcast(I32))
+            return plane
+
+        def load_words(name, words, width):
+            tile = sb(name, [P, width], U32)
+            nc.sync.dma_start(tile[:].bitcast(I32), words[0].rearrange("p n r -> p (n r)").bitcast(I32))
+            return tile
+
+        def load_weight(name, w, c0, c1):
+            raw = sb(name, [P, PACK, c1 - c0], F32)
+            nc.sync.dma_start(raw[:], w.rearrange("(p j) c -> p j c", j=PACK)[:, :, c0:c1])
+            return raw
+
+        def deal(name, raw, width, split):
+            m = width // PACK
+            dealt = sb(name, [P, PACK, m, PACK], BF16)
+            dst = dealt[:].rearrange("p t m j -> p m j t")
+            src = raw[:].rearrange("p j (m t) -> p m j t", t=PACK)
+            if split > 0:
+                nc.vector.tensor_copy(dst[:, :split], src[:, :split])
+            if split < m:
+                nc.scalar.copy(dst[:, split:], src[:, split:])
+            return dealt
+
+        def planes(name, width):
+            return sb(name + "_codes", [P, width], U32), sb(name + "_scales", [P, width], U8)
+
+        def quantize(codes, scales, values):
+            nc.vector.quantize_mx(out=codes.bitcast(FP8X4), scales=scales, in_=values)
+
+        def gather(name, window, dtype, d):
+            picked = sb(name, [P, V], dtype)
+            nc.vector.tensor_copy(picked[:], window[:].indirect(offsets[:, d * LIST_COLS : (d + 1) * LIST_COLS]))
+            return picked
+
+        def product(out, w_planes, t, codes, scales):
+            cols = slice(t * P, (t + 1) * P)
+            nc.tensor.matmul_mx(
+                out=out,
+                lhsT=w_planes[0][:, cols].bitcast(FP8X4),
+                lhsT_scale=w_planes[1][:, cols],
+                rhs=codes.bitcast(FP8X4),
+                rhs_scale=scales,
+                start=True,
+                stop=True,
+            )
+
+        def first_products(name, first_bank, w_planes, xw, xs):
+            banks = [bank("%s_%d" % (name, h), first_bank + h, PACK) for h in range(2)]
+            for h in range(2):
+                cols = slice(h * HALF, (h + 1) * HALF)
+                for t in range(PACK):
+                    product(banks[h][:, t, :], w_planes, t, xw[:, cols], xs[:, cols])
+            return banks
+
+        def woven(tile):
+            return tile[:].rearrange("p t v -> p v t")
+
+        xw_all = load_words("xw_all", x_words, T)
+        xs_all = load_scale_rows(nc.scalar, "xs_all", x_scales, T)
+
+        def load_halves(name, w):
+            return [load_weight("%s_%d" % (name, c), w, c * H // 2, (c + 1) * H // 2) for c in range(2)]
+
+        raw1 = load_halves("raw1", w1)
+        w4s_raw = load_scale_rows(nc.sync, "w4s_raw", w4_scales, H)
+        raw2 = load_halves("raw2", w2)
+        raw3 = load_halves("raw3", w3)
+        w4w_raw = load_words("w4w_raw", w4_words, H)
+
+        def quantize_half(name, q, raw, c, split):
+            dealt = deal("%s_%d" % (name, c), raw[c], H // 2, split)
+            for t in range(PACK):
+                cols = slice(t * P + c * P // 2, t * P + (c + 1) * P // 2)
+                quantize(q[0][:, cols], q[1][:, cols], dealt[:, t].rearrange("p m j -> p (m j)"))
+
+        xw = [gather("xw%d" % d, xw_all, U32, d) for d in range(3)]
+        xs = [gather("xs%d" % d, xs_all, U8, d) for d in range(3)]
+
+        q1 = planes("q1", H)
+        for c in range(2):
+            quantize_half("dealt1", q1, raw1, c, 0)
+        a1 = first_products("a1", 0, q1, xw[0], xs[0])
+
+        q4 = planes("q4", H)
+        nc.vector.tensor_copy(
+            q4[1][:].rearrange("p (t m) -> p m t", t=PACK), w4s_raw[:].rearrange("p (m t) -> p m t", t=PACK)
+        )
+
+        q2 = planes("q2", H)
+        for c in range(2):
+            quantize_half("dealt2", q2, raw2, c, (0, 64)[c])
+        a1s = [sb("a1s_%d" % h, [P, HALF, PACK], F32) for h in range(2)]
+        for h in range(2):
+            nc.scalar.copy(a1s[h][:], woven(a1[h]))
+        a2 = first_products("a2", 2, q2, xw[1], xs[1])
+
+        q3 = planes("q3", H)
+        for c in range(2):
+            quantize_half("dealt3", q3, raw3, c, (24, 40)[c])
+        a12 = [sb("a12_%d" % h, [P, HALF, PACK], F32) for h in range(2)]
+        for h in range(2):
+            nc.vector.tensor_tensor(a12[h][:], woven(a2[h]), a1s[h][:], MULT)
+        a3 = first_products("a3", 4, q3, xw[2], xs[2])
+
+        nc.scalar.copy(
+            q4[0][:].rearrange("p (t m) -> p m t", t=PACK), w4w_raw[:].rearrange("p (m t) -> p m t", t=PACK)
+        )
+
+        z = [sb("z_%d" % h, [P, HALF, PACK], BF16) for h in range(2)]
+        qz = [planes("qz_%d" % h, HALF) for h in range(2)]
+        for h in range(2):
+            nc.vector.tensor_tensor(z[h][:], woven(a3[h]), a12[h][:], MULT)
+        for h in range(2):
+            quantize(qz[h][0][:], qz[h][1][:], z[h][:].rearrange("p v t -> p (v t)"))
+
+        qo = planes("qo", V)
+        out_rows = out_0.rearrange("(p t) v -> p t v", t=PACK)
+        out_words = out_1[0].rearrange("p n r -> p (n r)").bitcast(I32)
+        for h in range(2):
+            cols = slice(h * HALF, (h + 1) * HALF)
+            y = sb("y_%d" % h, [P, PACK, HALF], F32)
+            for u in range(2):
+                o = bank("o_%d_%d" % (h, u), (6 + 2 * h + u) % 8, 2)
+                for e in range(2):
+                    product(o[:, e, :], q4, 2 * u + e, qz[h][0][:], qz[h][1][:])
+                nc.scalar.copy(y[:, 2 * u : 2 * u + 2, :], o[:])
+            nc.sync.dma_start(out_rows[:, :, cols], y[:])
+            yb = sb("yb_%d" % h, [P, HALF, PACK], BF16)
+            nc.vector.tensor_copy(
+                yb[:].rearrange("p (c i) t -> p c t i", i=4), y[:].rearrange("p t (c i) -> p c t i", i=4)
+            )
+            quantize(qo[0][:, cols], qo[1][:, cols], yb[:].rearrange("p v t -> p (v t)"))
+            nc.sync.dma_start(out_words[:, cols], qo[0][:, cols].bitcast(I32))
+        for q in range(4):
+            queue = (nc.sync, nc.scalar)[q % 2]
+            queue.dma_start(out_2[0, 4 * q : 4 * q + 4, :].bitcast(I32), qo[1][32 * q : 32 * q + 4, :].bitcast(I32))

@@ -28,8 +28,8 @@ def tile_picked_trilin_none_po_kernel(
         keep = ctx.enter_context(tc.tile_pool(name="keep", bufs=1))
         psum = ctx.enter_context(tc.psum_pool(name="psum", bufs=1))
 
-        def sb(name, shape, dtype):
-            return keep.tile(shape, dtype, name=name, align_bytes=64)
+        def sb(name, shape, dtype, tag=None):
+            return keep.tile(shape, dtype, name=name, tag=tag or name, align_bytes=64)
 
         def bank(name, index, slots):
             return psum.tile([P, slots, HALF], F32, name=name, tag="bank%d" % index)
@@ -37,11 +37,11 @@ def tile_picked_trilin_none_po_kernel(
         offsets = keep.tile([P, S // 16], U16, name="offsets")
         nc.sync.dma_start(offsets[:], offs)
 
-        def load_scale_rows(queue, name, rows, width):
+        def load_scale_rows(queues, name, rows, width):
             plane = sb(name, [P, width], U8)
             nc.vector.memset(plane[:].bitcast(I32), 0)
             for q in range(4):
-                queue.dma_start(plane[32 * q : 32 * q + 4, :].bitcast(I32), rows[0, 4 * q : 4 * q + 4, :].bitcast(I32))
+                queues[q % 2].dma_start(plane[32 * q : 32 * q + 4, :].bitcast(I32), rows[0, 4 * q : 4 * q + 4, :].bitcast(I32))
             return plane
 
         def load_words(name, words, width):
@@ -54,16 +54,14 @@ def tile_picked_trilin_none_po_kernel(
             nc.sync.dma_start(raw[:], w.rearrange("(p j) c -> p j c", j=PACK)[:, :, c0:c1])
             return raw
 
-        def deal(name, raw, width, split):
-            m = width // PACK
-            dealt = sb(name, [P, PACK, m, PACK], BF16)
-            dst = dealt[:].rearrange("p t m j -> p m j t")
-            src = raw[:].rearrange("p j (m t) -> p m j t", t=PACK)
+        def deal(dealt, raw, c, split):
+            m = H // 2 // PACK
+            dst = dealt[:, :, c * m : (c + 1) * m, :].rearrange("p t m j -> p m j t")
+            src = raw[c][:].rearrange("p j (m t) -> p m j t", t=PACK)
             if split > 0:
                 nc.vector.tensor_copy(dst[:, :split], src[:, :split])
             if split < m:
                 nc.scalar.copy(dst[:, split:], src[:, split:])
-            return dealt
 
         def planes(name, width):
             return sb(name + "_codes", [P, width], U32), sb(name + "_scales", [P, width], U8)
@@ -71,10 +69,10 @@ def tile_picked_trilin_none_po_kernel(
         def quantize(codes, scales, values):
             nc.vector.quantize_mx(out=codes.bitcast(FP8X4), scales=scales, in_=values)
 
-        def gather(name, window, dtype, d):
-            picked = sb(name, [P, V], dtype)
-            nc.vector.tensor_copy(picked[:], window[:].indirect(offsets[:, d * LIST_COLS : (d + 1) * LIST_COLS]))
-            return picked
+        def gather(name, window, dtype, tag=None):
+            picked = sb(name, [P, S], dtype, tag)
+            nc.vector.tensor_copy(picked[:], window[:].indirect(offsets[:]))
+            return [picked[:, d * V : (d + 1) * V] for d in range(3)]
 
         def product(out, w_planes, t, codes, scales):
             cols = slice(t * P, (t + 1) * P)
@@ -99,63 +97,68 @@ def tile_picked_trilin_none_po_kernel(
         def woven(tile):
             return tile[:].rearrange("p t v -> p v t")
 
+        def load_half(name, w, c):
+            return load_weight("%s_%d" % (name, c), w, c * H // 2, (c + 1) * H // 2)
+
+        xs_rows = sb("xs_rows", [P, T], U8)
+        xs_all = sb("xs_all", [P, T], U8)
+        nc.vector.memset(xs_all[:].bitcast(I32), 0)
+        for q in range(4):
+            live = slice(32 * q, 32 * q + 4)
+            queue = nc.sync if q < 2 else nc.scalar
+            queue.dma_start(xs_rows[live, :].bitcast(I32), x_scales[0, 4 * q : 4 * q + 4, :].bitcast(I32))
+            nc.vector.tensor_copy(xs_all[live, :].bitcast(I32), xs_rows[live, :].bitcast(I32))
+        raw1 = [load_half("raw1", w1, 0)]
         xw_all = load_words("xw_all", x_words, T)
-        xs_all = load_scale_rows(nc.scalar, "xs_all", x_scales, T)
-
-        def load_halves(name, w):
-            return [load_weight("%s_%d" % (name, c), w, c * H // 2, (c + 1) * H // 2) for c in range(2)]
-
-        raw1 = load_halves("raw1", w1)
-        w4s_raw = load_scale_rows(nc.sync, "w4s_raw", w4_scales, H)
-        raw2 = load_halves("raw2", w2)
-        raw3 = load_halves("raw3", w3)
+        raw1.append(load_half("raw1", w1, 1))
+        raw2 = [load_half("raw2", w2, c) for c in range(2)]
+        w4s_raw = load_scale_rows((nc.sync, nc.sync), "w4s_raw", w4_scales, H)
+        raw3 = [load_half("raw3", w3, c) for c in range(2)]
         w4w_raw = load_words("w4w_raw", w4_words, H)
 
-        def quantize_half(name, q, raw, c, split):
-            dealt = deal("%s_%d" % (name, c), raw[c], H // 2, split)
-            for t in range(PACK):
-                cols = slice(t * P + c * P // 2, t * P + (c + 1) * P // 2)
-                quantize(q[0][:, cols], q[1][:, cols], dealt[:, t].rearrange("p m j -> p (m j)"))
+        def quantize_weight(name, raw, splits, calls):
+            dealt = sb(name + "_dealt", [P, PACK, P, PACK], BF16)
+            for c in range(2):
+                deal(dealt, raw, c, splits[c])
+            q = planes(name, H)
+            flat = dealt[:].rearrange("p t m j -> p (t m j)")
+            width = H // calls
+            for i in range(calls):
+                cols = slice(i * width, (i + 1) * width)
+                quantize(q[0][:, cols], q[1][:, cols], flat[:, i * width * PACK : (i + 1) * width * PACK])
+            return q, dealt
 
-        xw = [gather("xw%d" % d, xw_all, U32, d) for d in range(3)]
-        xs = [gather("xs%d" % d, xs_all, U8, d) for d in range(3)]
+        xs = gather("xs", xs_all, U8)
+        xw = gather("xw", xw_all, U32)
 
-        q1 = planes("q1", H)
-        for c in range(2):
-            quantize_half("dealt1", q1, raw1, c, 0)
+        q1, dealt1 = quantize_weight("q1", raw1, (0, 0), 1)
         a1 = first_products("a1", 0, q1, xw[0], xs[0])
-
-        q4 = planes("q4", H)
-        nc.vector.tensor_copy(
-            q4[1][:].rearrange("p (t m) -> p m t", t=PACK), w4s_raw[:].rearrange("p (m t) -> p m t", t=PACK)
-        )
-
-        q2 = planes("q2", H)
-        for c in range(2):
-            quantize_half("dealt2", q2, raw2, c, (0, 64)[c])
+        q2, dealt2 = quantize_weight("q2", raw2, (0, 44), 2)
         a1s = [sb("a1s_%d" % h, [P, HALF, PACK], F32) for h in range(2)]
         for h in range(2):
             nc.scalar.copy(a1s[h][:], woven(a1[h]))
         a2 = first_products("a2", 2, q2, xw[1], xs[1])
 
-        q3 = planes("q3", H)
-        for c in range(2):
-            quantize_half("dealt3", q3, raw3, c, (24, 40)[c])
-        a12 = [sb("a12_%d" % h, [P, HALF, PACK], F32) for h in range(2)]
+        q3, dealt3 = quantize_weight("q3", raw3, (64, 16), 4)
+        a12 = [sb("a12_%d" % h, [P, HALF, PACK], F32, (None, "raw3_1")[h]) for h in range(2)]
         for h in range(2):
             nc.vector.tensor_tensor(a12[h][:], woven(a2[h]), a1s[h][:], MULT)
         a3 = first_products("a3", 4, q3, xw[2], xs[2])
 
+        q4 = sb("q4_codes", [P, H], U32), sb("q4_scales", [P, H], U8, tag="raw3_0")
         nc.scalar.copy(
             q4[0][:].rearrange("p (t m) -> p m t", t=PACK), w4w_raw[:].rearrange("p (m t) -> p m t", t=PACK)
         )
 
-        z = [sb("z_%d" % h, [P, HALF, PACK], BF16) for h in range(2)]
         qz = [planes("qz_%d" % h, HALF) for h in range(2)]
         for h in range(2):
-            nc.vector.tensor_tensor(z[h][:], woven(a3[h]), a12[h][:], MULT)
-        for h in range(2):
-            quantize(qz[h][0][:], qz[h][1][:], z[h][:].rearrange("p v t -> p (v t)"))
+            z = sb("z_%d" % h, [P, HALF, PACK], BF16, (None, "a12_0")[h])
+            nc.vector.tensor_tensor(z[:], woven(a3[h]), a12[h][:], MULT)
+            if h == 0:
+                nc.vector.tensor_copy(
+                    q4[1][:].rearrange("p (t m) -> p m t", t=PACK), w4s_raw[:].rearrange("p (m t) -> p m t", t=PACK)
+                )
+            quantize(qz[h][0][:], qz[h][1][:], z[:].rearrange("p v t -> p (v t)"))
 
         qo = planes("qo", V)
         out_rows = out_0.rearrange("(p t) v -> p t v", t=PACK)

@@ -35,14 +35,7 @@ def tile_picked_trilin_none_po_kernel(
             return psum.tile([P, slots, HALF], F32, name=name, tag="bank%d" % index)
 
         offsets = keep.tile([P, S // 16], U16, name="offsets")
-        nc.sync.dma_start(offsets[:], offs)
 
-        def load_scale_rows(queues, name, rows, width):
-            plane = sb(name, [P, width], U8)
-            nc.vector.memset(plane[:].bitcast(I32), 0)
-            for q in range(4):
-                queues[q % 2].dma_start(plane[32 * q : 32 * q + 4, :].bitcast(I32), rows[0, 4 * q : 4 * q + 4, :].bitcast(I32))
-            return plane
 
         def load_words(name, words, width):
             tile = sb(name, [P, width], U32)
@@ -69,10 +62,11 @@ def tile_picked_trilin_none_po_kernel(
         def quantize(codes, scales, values):
             nc.vector.quantize_mx(out=codes.bitcast(FP8X4), scales=scales, in_=values)
 
-        def gather(name, window, dtype, tag=None):
-            picked = sb(name, [P, S], dtype, tag)
-            nc.vector.tensor_copy(picked[:], window[:].indirect(offsets[:]))
-            return [picked[:, d * V : (d + 1) * V] for d in range(3)]
+        def gather(name, window, dtype, first, pieces, tag=None):
+            picked = sb(name, [P, pieces * V], dtype, tag)
+            entries = offsets[:, first * LIST_COLS : (first + pieces) * LIST_COLS]
+            nc.vector.tensor_copy(picked[:], window[:].indirect(entries))
+            return [picked[:, d * V : (d + 1) * V] for d in range(pieces)]
 
         def product(out, w_planes, t, codes, scales):
             cols = slice(t * P, (t + 1) * P)
@@ -100,6 +94,8 @@ def tile_picked_trilin_none_po_kernel(
         def load_half(name, w, c):
             return load_weight("%s_%d" % (name, c), w, c * H // 2, (c + 1) * H // 2)
 
+        w4s_raw = sb("w4s_raw", [P, H], U8)
+        nc.gpsimd.memset(w4s_raw[:].bitcast(I32), 0)
         xs_rows = sb("xs_rows", [P, T], U8)
         xs_all = sb("xs_all", [P, T], U8)
         nc.vector.memset(xs_all[:].bitcast(I32), 0)
@@ -109,12 +105,14 @@ def tile_picked_trilin_none_po_kernel(
             queue.dma_start(xs_rows[live, :].bitcast(I32), x_scales[0, 4 * q : 4 * q + 4, :].bitcast(I32))
             nc.vector.tensor_copy(xs_all[live, :].bitcast(I32), xs_rows[live, :].bitcast(I32))
         raw1 = [load_half("raw1", w1, 0)]
+        nc.sync.dma_start(offsets[:], offs)
         xw_all = load_words("xw_all", x_words, T)
         raw1.append(load_half("raw1", w1, 1))
         raw2 = [load_half("raw2", w2, c) for c in range(2)]
-        w4s_raw = load_scale_rows((nc.sync, nc.sync), "w4s_raw", w4_scales, H)
         raw3 = [load_half("raw3", w3, c) for c in range(2)]
         w4w_raw = load_words("w4w_raw", w4_words, H)
+        for q in range(4):
+            nc.sync.dma_start(w4s_raw[32 * q : 32 * q + 4, :].bitcast(I32), w4_scales[0, 4 * q : 4 * q + 4, :].bitcast(I32))
 
         def quantize_weight(name, raw, splits, calls):
             dealt = sb(name + "_dealt", [P, PACK, P, PACK], BF16)
@@ -128,36 +126,38 @@ def tile_picked_trilin_none_po_kernel(
                 quantize(q[0][:, cols], q[1][:, cols], flat[:, i * width * PACK : (i + 1) * width * PACK])
             return q, dealt
 
-        xs = gather("xs", xs_all, U8)
-        xw = gather("xw", xw_all, U32)
+        xs = gather("xs", xs_all, U8, 0, 3)
+        xw = gather("xw", xw_all, U32, 0, 3)
 
         q1, dealt1 = quantize_weight("q1", raw1, (0, 0), 1)
         a1 = first_products("a1", 0, q1, xw[0], xs[0])
-        q2, dealt2 = quantize_weight("q2", raw2, (0, 44), 2)
-        a1s = [sb("a1s_%d" % h, [P, HALF, PACK], F32) for h in range(2)]
+        q2, dealt2 = quantize_weight("q2", raw2, (0, 40), 2)
+        a1s = sb("a1s", [P, 2, HALF, PACK], F32, tag="raw2_1")
         for h in range(2):
-            nc.scalar.copy(a1s[h][:], woven(a1[h]))
+            nc.scalar.copy(a1s[:, h], woven(a1[h]))
         a2 = first_products("a2", 2, q2, xw[1], xs[1])
 
-        q3, dealt3 = quantize_weight("q3", raw3, (64, 16), 4)
-        a12 = [sb("a12_%d" % h, [P, HALF, PACK], F32, (None, "raw3_1")[h]) for h in range(2)]
-        for h in range(2):
-            nc.vector.tensor_tensor(a12[h][:], woven(a2[h]), a1s[h][:], MULT)
-        a3 = first_products("a3", 4, q3, xw[2], xs[2])
-
-        q4 = sb("q4_codes", [P, H], U32), sb("q4_scales", [P, H], U8, tag="raw3_0")
+        q3, dealt3 = quantize_weight("q3", raw3, (64, 28), 4)
+        q4 = sb("q4_codes", [P, H], U32), sb("q4_scales", [P, H], U8, tag="q3_dealt")
         nc.scalar.copy(
             q4[0][:].rearrange("p (t m) -> p m t", t=PACK), w4w_raw[:].rearrange("p (m t) -> p m t", t=PACK)
         )
 
+        a12 = [sb("a12_%d" % h, [P, HALF, PACK], F32, (None, "w4w_raw")[h]) for h in range(2)]
+        for h in range(2):
+            nc.vector.tensor_tensor(a12[h][:], woven(a2[h]), a1s[:, h], MULT)
+        a3 = first_products("a3", 4, q3, xw[2], xs[2])
+
+        nc.gpsimd.tensor_copy(
+            q4[1][:].rearrange("p (t m) -> p t m", t=PACK), w4s_raw[:].rearrange("p (m t) -> p t m", t=PACK)
+        )
+
         qz = [planes("qz_%d" % h, HALF) for h in range(2)]
         for h in range(2):
-            z = sb("z_%d" % h, [P, HALF, PACK], BF16, (None, "a12_0")[h])
-            nc.vector.tensor_tensor(z[:], woven(a3[h]), a12[h][:], MULT)
-            if h == 0:
-                nc.vector.tensor_copy(
-                    q4[1][:].rearrange("p (t m) -> p m t", t=PACK), w4s_raw[:].rearrange("p (m t) -> p m t", t=PACK)
-                )
+            z = sb("z_%d" % h, [P, HALF, PACK], BF16)
+            for part in range(h + 1):
+                cols = slice(part * HALF // (h + 1), (part + 1) * HALF // (h + 1))
+                nc.vector.tensor_tensor(z[:, cols], woven(a3[h])[:, cols], a12[h][:, cols], MULT)
             quantize(qz[h][0][:], qz[h][1][:], z[:].rearrange("p v t -> p (v t)"))
 
         qo = planes("qo", V)
@@ -170,7 +170,10 @@ def tile_picked_trilin_none_po_kernel(
                 o = bank("o_%d_%d" % (h, u), (6 + 2 * h + u) % 8, 2)
                 for e in range(2):
                     product(o[:, e, :], q4, 2 * u + e, qz[h][0][:], qz[h][1][:])
-                nc.scalar.copy(y[:, 2 * u : 2 * u + 2, :], o[:])
+                if (h, u) == (0, 1):
+                    nc.vector.tensor_copy(y[:, 2 * u : 2 * u + 2, :], o[:])
+                else:
+                    nc.scalar.copy(y[:, 2 * u : 2 * u + 2, :], o[:])
             nc.sync.dma_start(out_rows[:, :, cols], y[:])
             yb = sb("yb_%d" % h, [P, HALF, PACK], BF16)
             nc.vector.tensor_copy(

from contextlib import ExitStack

import concourse.mybir as mybir

K, T, S, V, H = 512, 1024, 768, 256, 512
FLOPS = 3 * 2 * K * H * V + 2 * H * H * V

F32 = mybir.dt.float32
BF16 = mybir.dt.bfloat16
I32 = mybir.dt.int32
U32 = mybir.dt.uint32
U16 = mybir.dt.uint16
U8 = mybir.dt.uint8
FP8X4 = mybir.dt.float8_e4m3fn_x4
MULT = mybir.AluOpType.mult

P = 128
PACK = 4
HALF = V // 2
LIST_COLS = V // 16


def tile_picked_trilin_none_po_kernel(
    tc, x_words, x_scales, w1, w2, w3, w4_words, w4_scales, offs, out_0, out_1, out_2
):
    nc = tc.nc
    with ExitStack() as ctx:
        keep = ctx.enter_context(tc.tile_pool(name="keep", bufs=1))
        psum = ctx.enter_context(tc.psum_pool(name="psum", bufs=1))

        def sb(name, shape, dtype, tag=None):
            return keep.tile(shape, dtype, name=name, tag=tag or name, align_bytes=64)

        def bank(name, index, slots):
            return psum.tile([P, slots, HALF], F32, name=name, tag="bank%d" % index)

        offsets = keep.tile([P, S // 16], U16, name="offsets")


        def load_words(name, words, width):
            tile = sb(name, [P, width], U32)
            nc.sync.dma_start(tile[:].bitcast(I32), words[0].rearrange("p n r -> p (n r)").bitcast(I32))
            return tile

        def load_weight(name, w, c0, c1):
            raw = sb(name, [P, PACK, c1 - c0], F32)
            nc.sync.dma_start(raw[:], w.rearrange("(p j) c -> p j c", j=PACK)[:, :, c0:c1])
            return raw

        def deal(dealt, raw, c, split):
            m = H // 2 // PACK
            dst = dealt[:, :, c * m : (c + 1) * m, :].rearrange("p t m j -> p m j t")
            src = raw[c][:].rearrange("p j (m t) -> p m j t", t=PACK)
            if split > 0:
                nc.vector.tensor_copy(dst[:, :split], src[:, :split])
            if split < m:
                nc.scalar.copy(dst[:, split:], src[:, split:])

        def planes(name, width):
            return sb(name + "_codes", [P, width], U32), sb(name + "_scales", [P, width], U8)

        def quantize(codes, scales, values):
            nc.vector.quantize_mx(out=codes.bitcast(FP8X4), scales=scales, in_=values)

        def gather(name, window, dtype, first, pieces, tag=None):
            picked = sb(name, [P, pieces * V], dtype, tag)
            entries = offsets[:, first * LIST_COLS : (first + pieces) * LIST_COLS]
            nc.vector.tensor_copy(picked[:], window[:].indirect(entries))
            return [picked[:, d * V : (d + 1) * V] for d in range(pieces)]

        def product(out, w_planes, t, codes, scales):
            cols = slice(t * P, (t + 1) * P)
            nc.tensor.matmul_mx(
                out=out,
                lhsT=w_planes[0][:, cols].bitcast(FP8X4),
                lhsT_scale=w_planes[1][:, cols],
                rhs=codes.bitcast(FP8X4),
                rhs_scale=scales,
                start=True,
                stop=True,
            )

        def first_products(name, first_bank, w_planes, xw, xs):
            banks = [bank("%s_%d" % (name, h), first_bank + h, PACK) for h in range(2)]
            for h in range(2):
                cols = slice(h * HALF, (h + 1) * HALF)
                for t in range(PACK):
                    product(banks[h][:, t, :], w_planes, t, xw[:, cols], xs[:, cols])
            return banks

        def woven(tile):
            return tile[:].rearrange("p t v -> p v t")

        def load_half(name, w, c):
            return load_weight("%s_%d" % (name, c), w, c * H // 2, (c + 1) * H // 2)

        w4s_raw = sb("w4s_raw", [P, H], U8)
        nc.gpsimd.memset(w4s_raw[:].bitcast(I32), 0)
        xs_rows = sb("xs_rows", [P, T], U8)
        xs_all = sb("xs_all", [P, T], U8)
        nc.vector.memset(xs_all[:].bitcast(I32), 0)
        for q in range(4):
            live = slice(32 * q, 32 * q + 4)
            queue = nc.sync if q < 2 else nc.scalar
            queue.dma_start(xs_rows[live, :].bitcast(I32), x_scales[0, 4 * q : 4 * q + 4, :].bitcast(I32))
            nc.vector.tensor_copy(xs_all[live, :].bitcast(I32), xs_rows[live, :].bitcast(I32))
        raw1 = [load_half("raw1", w1, 0)]
        nc.sync.dma_start(offsets[:], offs)
        xw_all = load_words("xw_all", x_words, T)
        raw1.append(load_half("raw1", w1, 1))
        raw2 = [load_half("raw2", w2, c) for c in range(2)]
        raw3 = [load_half("raw3", w3, c) for c in range(2)]
        w4w_raw = load_words("w4w_raw", w4_words, H)
        for q in range(4):
            nc.sync.dma_start(w4s_raw[32 * q : 32 * q + 4, :].bitcast(I32), w4_scales[0, 4 * q : 4 * q + 4, :].bitcast(I32))

        def quantize_weight(name, raw, splits, calls):
            dealt = sb(name + "_dealt", [P, PACK, P, PACK], BF16)
            for c in range(2):
                deal(dealt, raw, c, splits[c])
            q = planes(name, H)
            flat = dealt[:].rearrange("p t m j -> p (t m j)")
            width = H // calls
            for i in range(calls):
                cols = slice(i * width, (i + 1) * width)
                quantize(q[0][:, cols], q[1][:, cols], flat[:, i * width * PACK : (i + 1) * width * PACK])
            return q, dealt

        xs = gather("xs", xs_all, U8, 0, 3)
        xw = gather("xw", xw_all, U32, 0, 3)

        q1, dealt1 = quantize_weight("q1", raw1, (0, 0), 1)
        a1 = first_products("a1", 0, q1, xw[0], xs[0])
        q2, dealt2 = quantize_weight("q2", raw2, (0, 40), 2)
        a1s = sb("a1s", [P, 2, HALF, PACK], F32, tag="raw2_1")
        for h in range(2):
            nc.scalar.copy(a1s[:, h], woven(a1[h]))
        a2 = first_products("a2", 2, q2, xw[1], xs[1])

        q3, dealt3 = quantize_weight("q3", raw3, (64, 28), 4)
        q4 = sb("q4_codes", [P, H], U32), sb("q4_scales", [P, H], U8, tag="q3_dealt")
        nc.scalar.copy(
            q4[0][:].rearrange("p (t m) -> p m t", t=PACK), w4w_raw[:].rearrange("p (m t) -> p m t", t=PACK)
        )

        a12 = [sb("a12_%d" % h, [P, HALF, PACK], F32, (None, "w4w_raw")[h]) for h in range(2)]
        for h in range(2):
            nc.vector.tensor_tensor(a12[h][:], woven(a2[h]), a1s[:, h], MULT)
        a3 = first_products("a3", 4, q3, xw[2], xs[2])

        nc.gpsimd.tensor_copy(
            q4[1][:].rearrange("p (t m) -> p t m", t=PACK), w4s_raw[:].rearrange("p (m t) -> p t m", t=PACK)
        )

        qz = [planes("qz_%d" % h, HALF) for h in range(2)]
        for h in range(2):
            z = sb("z_%d" % h, [P, HALF, PACK], BF16)
            for part in range(h + 1):
                cols = slice(part * HALF // (h + 1), (part + 1) * HALF // (h + 1))
                nc.vector.tensor_tensor(z[:, cols], woven(a3[h])[:, cols], a12[h][:, cols], MULT)
            quantize(qz[h][0][:], qz[h][1][:], z[:].rearrange("p v t -> p (v t)"))

        qo = planes("qo", V)
        out_rows = out_0.rearrange("(p t) v -> p t v", t=PACK)
        out_words = out_1[0].rearrange("p n r -> p (n r)").bitcast(I32)
        for h in range(2):
            cols = slice(h * HALF, (h + 1) * HALF)
            y = sb("y_%d" % h, [P, PACK, HALF], F32)
            for u in range(2):
                o = bank("o_%d_%d" % (h, u), (6 + 2 * h + u) % 8, 2)
                for e in range(2):
                    product(o[:, e, :], q4, 2 * u + e, qz[h][0][:], qz[h][1][:])
                if (h, u) == (0, 1):
                    nc.vector.tensor_copy(y[:, 2 * u : 2 * u + 2, :], o[:])
                else:
                    nc.scalar.copy(y[:, 2 * u : 2 * u + 2, :], o[:])
            nc.sync.dma_start(out_rows[:, :, cols], y[:])
            yb = sb("yb_%d" % h, [P, HALF, PACK], BF16)
            nc.vector.tensor_copy(
                yb[:].rearrange("p (c i) t -> p c t i", i=4), y[:].rearrange("p t (c i) -> p c t i", i=4)
            )
            quantize(qo[0][:, cols], qo[1][:, cols], yb[:].rearrange("p v t -> p (v t)"))
            nc.sync.dma_start(out_words[:, cols], qo[0][:, cols].bitcast(I32))
        for q in range(4):
            queue = (nc.sync, nc.scalar)[q % 2]
            queue.dma_start(out_2[0, 4 * q : 4 * q + 4, :].bitcast(I32), qo[1][32 * q : 32 * q + 4, :].bitcast(I32))
